import numpy as np
import ml_dtypes


def mxq(x, axis, fmt="e4m3"):
    dtype, down = {"e4m3": (ml_dtypes.float8_e4m3fn, 7), "e5m2": (ml_dtypes.float8_e5m2, 14)}[fmt]
    v = np.moveaxis(np.asarray(x, np.float32).astype(ml_dtypes.bfloat16).astype(np.float64), axis, -1)
    blocks = v.reshape(v.shape[:-1] + (-1, 32))
    amax = np.abs(blocks).max(-1, keepdims=True)
    byte = np.maximum(np.where(amax > 0, np.frexp(amax)[1] - 1 + 127, 0) - down, 1)
    scale = np.exp2(byte - 127.0)
    codes = (blocks / scale).astype(np.float32).astype(dtype).astype(np.float64)
    return np.moveaxis((codes * scale).reshape(v.shape), -1, axis)


WIDE = False


def mx_kscale(k):
    if not WIDE:
        return np.ones(k)
    levels = np.array([10, -10, 5, -5, 0])
    if k % 512:
        return np.exp2(np.random.permutation(np.resize(levels, k // 32))).repeat(32)
    a = np.empty((k // 512, 16))
    for p in range(k // 512):
        a[p, :8] = np.random.permutation(np.resize(levels, 8))
        for g in range(8):
            far = levels[np.abs(levels - a[p, g]) >= 10]
            a[p, g + 8] = far[np.random.randint(len(far))]
    return np.exp2(a.ravel()).repeat(32)


def f64(x):
    return np.asarray(x).astype(np.float64)


def striped(idx):
    return np.tile(idx.reshape(-1, 16).T, (8, 1)).astype(np.uint16)


def unstriped(offs):
    return offs[:16].T.reshape(-1).astype(np.int64)


def silu(v):
    return v / (1.0 + np.exp(-np.maximum(v, -700.0)))


K, T, H, N = 512, 128, 512, 512


def setup_inputs():
    n = np.random.standard_normal
    s = mx_kscale(K)[:, None]
    u = mx_kscale(H)
    idx = np.random.permutation(H)
    v = np.empty(H)
    v[idx] = u
    return {
        "xT": (n((K, T)) * s).astype(np.float32),
        "w1": (n((K, H)) / np.sqrt(K) / s * v).astype(np.float32),
        "w2": (n((H, N)) / np.sqrt(H) / u[:, None]).astype(np.float32),
        "offs": striped(idx),
    }


def reference(xT, w1, w2, offs):
    idx = unstriped(offs)
    h = silu(mxq(f64(w1), 0, "e4m3").T @ mxq(f64(xT), 0, "e4m3"))
    return mxq(f64(w2), 0, "e4m3").T @ mxq(h[idx], 0, "e4m3")

@@ -1,0 +1,171 @@
+from contextlib import ExitStack
+
+import concourse.mybir as mybir
+from concourse.masks import make_identity
+
+K, T, H, N = 512, 128, 512, 512
+FLOPS = 2 * T * H * (K + N)
+
+F32 = mybir.dt.float32
+BF16 = mybir.dt.bfloat16
+U32 = mybir.dt.uint32
+U16 = mybir.dt.uint16
+U8 = mybir.dt.uint8
+FP8X4 = mybir.dt.float8_e4m3fn_x4
+SILU = mybir.ActivationFunctionType.Silu
+COPY = mybir.ActivationFunctionType.Copy
+
+P = 128
+PACK = 4
+
+W1_LOADS = (320, 192)
+W1_CHUNKS = ((0, 256, (("v", 176), ("s", 80))), (256, 64, (("v", 44), ("s", 20))), (320, 128, (("v", 80), ("s", 48))), (448, 64, (("v", 32), ("s", 32))))
+W2_LOADS = (256, 256)
+W2_CHUNKS = ((0, 256, (("g", 128), ("g", 128))), (256, 256, (("v", 160), ("s", 96))))
+V_GATHER = 288
+BANKS = ("acc0", "acc256", "acc320", "acc2_3")
+
+
+def tile_picked_shuffle_mlp_silu_perm_l_kernel(tc, xT, w1, w2, offs, out):
+    nc = tc.nc
+    with ExitStack() as ctx:
+        keep = ctx.enter_context(tc.tile_pool(name="keep", bufs=1))
+        psum = ctx.enter_context(tc.psum_pool(name="psum", bufs=1))
+
+        def load(dram, widths, name):
+            raws = []
+            c0 = 0
+            for i, width in enumerate(widths):
+                raw = keep.tile([P, PACK, width], F32, name=f"{name}_raw{i}")
+                nc.sync.dma_start(raw[:], dram[:, c0 : c0 + width].rearrange("(p j) w -> p j w", j=PACK))
+                raws.append(raw)
+                c0 += width
+            return raws
+
+        offsets = keep.tile([P, H // 16], U16, name="offsets")
+        x_raw = load(xT, (T,), "x")
+        w1_raw = load(w1, W1_LOADS, "w1")
+        nc.sync.dma_start(offsets[:], offs)
+        w2_raw = load(w2, W2_LOADS, "w2")
+
+        warm = keep.tile([P, 1], F32, name="warm")
+        nc.vector.memset(warm[:], 0.0)
+        nc.scalar.activation(warm[:], warm[:], SILU)
+        ident = keep.tile([P, P], F32, name="ident")
+        make_identity(nc, ident[:])
+
+        def chunk_codes(raws, loads, chunk, name, codes, scales):
+            c0, width, shares = chunk
+            first = 0
+            which = 0
+            while c0 >= first + loads[which]:
+                first += loads[which]
+                which += 1
+            src = raws[which][:].rearrange("p j w -> p w j")
+            grouped = keep.tile([P, width, PACK], BF16, name=f"{name}_grouped{c0}", align_bytes=64)
+            a = 0
+            for engine, share in shares:
+                dst = grouped[:, a : a + share, :]
+                part = src[:, c0 - first + a : c0 - first + a + share, :]
+                if engine == "v":
+                    nc.vector.tensor_copy(out=dst, in_=part)
+                elif engine == "s":
+                    nc.scalar.copy(out=dst, in_=part)
+                else:
+                    nc.gpsimd.tensor_scalar(
+                        out=dst, in0=part, scalar1=1.0, scalar2=0.0, op0=mybir.AluOpType.mult, op1=mybir.AluOpType.add
+                    )
+                a += share
+            quantize(grouped[:], codes[:, c0 : c0 + width], scales[:, c0 : c0 + width])
+
+        def quantize(grouped, codes, scales):
+            nc.vector.quantize_mx(
+                out=codes.bitcast(FP8X4), scales=scales, in_=grouped.rearrange("p w j -> p (w j)")
+            )
+
+        junk = psum.tile([P, 4, P], F32, name="junk")
+
+        def warm_up(raw, c):
+            for j in range(PACK):
+                nc.tensor.transpose(junk[:, j, :], raw[:, j, c : c + P], ident[:])
+
+        x_codes = keep.tile([P, T], U32, name="x_codes", align_bytes=64)
+        x_scales = keep.tile([P, T], U8, name="x_scales", align_bytes=64)
+        chunk_codes(x_raw, (T,), (0, T, (("v", 128),)), "x", x_codes, x_scales)
+
+        w1_codes = keep.tile([P, H], U32, name="w1_codes", align_bytes=64)
+        w1_scales = keep.tile([P, H], U8, name="w1_scales", align_bytes=64)
+        h = keep.tile([P, H], F32, name="h", align_bytes=64)
+        h16 = keep.tile([P, H], BF16, name="h16", align_bytes=64)
+        accs = []
+        for chunk in W1_CHUNKS:
+            c0, width, shares = chunk
+            cols = slice(c0, c0 + width)
+            chunk_codes(w1_raw, W1_LOADS, chunk, "w1", w1_codes, w1_scales)
+            acc = psum.tile([P, width], F32, name=f"acc{c0}")
+            accs.append((cols, acc))
+            nc.tensor.matmul_mx(
+                out=acc[:],
+                lhsT=x_codes[:].bitcast(FP8X4),
+                lhsT_scale=x_scales[:],
+                rhs=w1_codes[:, cols].bitcast(FP8X4),
+                rhs_scale=w1_scales[:, cols],
+                start=True,
+                stop=True,
+            )
+            nc.scalar.activation(h[:, cols], acc[:], SILU)
+
+        for cols, acc in accs:
+            nc.scalar.activation(h16[:, cols], acc[:], SILU)
+        warm_up(w2_raw[0], 0)
+        warm_up(w2_raw[0], P)
+        picked = keep.tile([P, H], BF16, name="picked", align_bytes=64)
+        ordered = picked[:].rearrange("q (u p e) -> q p u e", u=2, e=2)
+        nc.vector.tensor_copy(
+            ordered[:, 0 : V_GATHER // PACK], h[:].indirect(offsets[:, 0 : V_GATHER // 16])
+        )
+        if V_GATHER < H:
+            nc.scalar.activation(
+                ordered[:, V_GATHER // PACK : P], h16[:].indirect(offsets[:, V_GATHER // 16 : H // 16]), COPY
+            )
+
+        turned = psum.tile([P, 2, T], F32, name="turned")
+        words = picked[:].bitcast(F32)
+        for u in range(2):
+            nc.tensor.transpose(turned[:, u, :], words[:, u * P : (u + 1) * P], ident[:])
+        h_grouped = keep.tile([P, T, PACK], BF16, name="h_grouped", align_bytes=64)
+        nc.scalar.copy(
+            out=h_grouped[:].rearrange("p t j -> p (t j)").bitcast(F32).rearrange("p (t u) -> p t u", u=2),
+            in_=turned[:].rearrange("p u t -> p t u"),
+        )
+        h_codes = keep.tile([P, T], U32, name="h_codes", align_bytes=64)
+        h_scales = keep.tile([P, T], U8, name="h_scales", align_bytes=64)
+        quantize(h_grouped[:], h_codes[:], h_scales[:])
+
+        w2_codes = keep.tile([P, N], U32, name="w2_codes", align_bytes=64)
+        w2_scales = keep.tile([P, N], U8, name="w2_scales", align_bytes=64)
+        for chunk in W2_CHUNKS:
+            chunk_codes(w2_raw, W2_LOADS, chunk, "w2", w2_codes, w2_scales)
+
+        blocks = N // P
+        results = keep.tile([P, blocks, T], F32, name="results")
+        for b in range(blocks):
+            m = slice(b * P, (b + 1) * P)
+            acc2 = psum.tile([P, T], F32, name=f"acc2_{b}", tag=BANKS[b])
+            nc.tensor.matmul_mx(
+                out=acc2[:],
+                lhsT=w2_codes[:, m].bitcast(FP8X4),
+                lhsT_scale=w2_scales[:, m],
+                rhs=h_codes[:].bitcast(FP8X4),
+                rhs_scale=h_scales[:],
+                start=True,
+                stop=True,
+            )
+            if b % 2 == 0:
+                nc.vector.tensor_copy(out=results[:, b, :], in_=acc2[:])
+            else:
+                nc.scalar.copy(out=results[:, b, :], in_=acc2[:])
+        rows = out.rearrange("(b p) t -> p b t", p=P)
+        nc.sync.dma_start(rows[:, 0:2, :], results[:, 0:2, :])
+        nc.sync.dma_start(rows[:, 2:3, :], results[:, 2:3, :])
+        nc.scalar.dma_start(rows[:, 3:4, :], results[:, 3:4, :])

@@ -48,9 +48,6 @@ def tile_picked_shuffle_mlp_silu_perm_l_kernel(tc, xT, w1, w2, offs, out):
         nc.sync.dma_start(offsets[:], offs)
         w2_raw = load(w2, W2_LOADS, "w2")
 
-        warm = keep.tile([P, 1], F32, name="warm")
-        nc.vector.memset(warm[:], 0.0)
-        nc.scalar.activation(warm[:], warm[:], SILU)
         ident = keep.tile([P, P], F32, name="ident")
         make_identity(nc, ident[:])
 
@@ -83,12 +80,6 @@ def tile_picked_shuffle_mlp_silu_perm_l_kernel(tc, xT, w1, w2, offs, out):
                 out=codes.bitcast(FP8X4), scales=scales, in_=grouped.rearrange("p w j -> p (w j)")
             )
 
-        junk = psum.tile([P, 4, P], F32, name="junk")
-
-        def warm_up(raw, c):
-            for j in range(PACK):
-                nc.tensor.transpose(junk[:, j, :], raw[:, j, c : c + P], ident[:])
-
         x_codes = keep.tile([P, T], U32, name="x_codes", align_bytes=64)
         x_scales = keep.tile([P, T], U8, name="x_scales", align_bytes=64)
         chunk_codes(x_raw, (T,), (0, T, (("v", 128),)), "x", x_codes, x_scales)
@@ -117,8 +108,6 @@ def tile_picked_shuffle_mlp_silu_perm_l_kernel(tc, xT, w1, w2, offs, out):
 
         for cols, acc in accs:
             nc.scalar.activation(h16[:, cols], acc[:], SILU)
-        warm_up(w2_raw[0], 0)
-        warm_up(w2_raw[0], P)
         picked = keep.tile([P, H], BF16, name="picked", align_bytes=64)
         ordered = picked[:].rearrange("q (u p e) -> q p u e", u=2, e=2)
         nc.vector.tensor_copy(

@@ -17,144 +17,150 @@ COPY = mybir.ActivationFunctionType.Copy
 
 P = 128
 PACK = 4
+LINE = 4
 
-W1_LOADS = (320, 192)
-W1_CHUNKS = ((0, 256, (("v", 176), ("s", 80))), (256, 64, (("v", 44), ("s", 20))), (320, 128, (("v", 80), ("s", 48))), (448, 64, (("v", 32), ("s", 32))))
-W2_LOADS = (256, 256)
-W2_CHUNKS = ((0, 256, (("g", 128), ("g", 128))), (256, 256, (("v", 160), ("s", 96))))
-V_GATHER = 288
-BANKS = ("acc0", "acc256", "acc320", "acc2_3")
+X_LOADS = (128,)
+X_PIECES = ((("vector", 128),),)
+W1_LOADS = (128, 128, 128, 128)
+W1_PIECES = ((("scalar", 128),), (("vector", 128),), (("scalar", 128),), (("vector", 128),),)
+W2_LOADS = (128, 128, 256)
+W2_PIECES = ((("vector", 128),), (("gpsimd", 128),), (("vector", 160), ("scalar", 96),),)
+REUSED = {"w2256_grouped": 0, "h": 1536, "w2128_scales": 2048}
+V_GATHER = 256
 
 
 def tile_picked_shuffle_mlp_silu_perm_l_kernel(tc, xT, w1, w2, offs, out):
     nc = tc.nc
     with ExitStack() as ctx:
         keep = ctx.enter_context(tc.tile_pool(name="keep", bufs=1))
+        reuse = ctx.enter_context(tc.tile_pool(name="reuse", bufs=1))
         psum = ctx.enter_context(tc.psum_pool(name="psum", bufs=1))
+
+        def tile(shape, dtype, name):
+            if name in REUSED:
+                return reuse.tile(shape, dtype, name=name, offset=REUSED[name], align_bytes=64)
+            return keep.tile(shape, dtype, name=name, align_bytes=64)
 
         def load(dram, widths, name):
             raws = []
             c0 = 0
-            for i, width in enumerate(widths):
-                raw = keep.tile([P, PACK, width], F32, name=f"{name}_raw{i}")
+            for width in widths:
+                raw = tile([P, PACK, width], F32, f"{name}_raw{c0}")
                 nc.sync.dma_start(raw[:], dram[:, c0 : c0 + width].rearrange("(p j) w -> p j w", j=PACK))
-                raws.append(raw)
+                raws.append((c0, width, raw))
                 c0 += width
             return raws
 
         offsets = keep.tile([P, H // 16], U16, name="offsets")
-        x_raw = load(xT, (T,), "x")
+        x_raw = load(xT, X_LOADS, "x")
         w1_raw = load(w1, W1_LOADS, "w1")
         nc.sync.dma_start(offsets[:], offs)
         w2_raw = load(w2, W2_LOADS, "w2")
 
+        warm = keep.tile([P, 1], F32, name="warm")
+        nc.vector.memset(warm[:], 0.0)
+        nc.scalar.activation(warm[:], warm[:], SILU)
         ident = keep.tile([P, P], F32, name="ident")
         make_identity(nc, ident[:])
 
-        def chunk_codes(raws, loads, chunk, name, codes, scales):
-            c0, width, shares = chunk
-            first = 0
-            which = 0
-            while c0 >= first + loads[which]:
-                first += loads[which]
-                which += 1
-            src = raws[which][:].rearrange("p j w -> p w j")
-            grouped = keep.tile([P, width, PACK], BF16, name=f"{name}_grouped{c0}", align_bytes=64)
+        def round_and_group(name, raws, c0, copies):
+            grouped = tile([P, sum(share for engine, share in copies), PACK], BF16, f"{name}{c0}_grouped")
             a = 0
-            for engine, share in shares:
+            for engine, share in copies:
+                first, width, raw = [r for r in raws if r[0] <= c0 + a < r[0] + r[1]][0]
                 dst = grouped[:, a : a + share, :]
-                part = src[:, c0 - first + a : c0 - first + a + share, :]
-                if engine == "v":
-                    nc.vector.tensor_copy(out=dst, in_=part)
-                elif engine == "s":
-                    nc.scalar.copy(out=dst, in_=part)
-                else:
+                src = raw[:, :, c0 + a - first : c0 + a - first + share]
+                if engine == "gpsimd":
                     nc.gpsimd.tensor_scalar(
-                        out=dst, in0=part, scalar1=1.0, scalar2=0.0, op0=mybir.AluOpType.mult, op1=mybir.AluOpType.add
+                        out=dst,
+                        in0=src.rearrange("p j w -> p w j"),
+                        scalar1=1.0,
+                        scalar2=0.0,
+                        op0=mybir.AluOpType.mult,
+                        op1=mybir.AluOpType.add,
                     )
+                else:
+                    dst = dst.rearrange("p (c i) j -> p c j i", i=LINE)
+                    src = src.rearrange("p j (c i) -> p c j i", i=LINE)
+                    if engine == "vector":
+                        nc.vector.tensor_copy(out=dst, in_=src)
+                    else:
+                        nc.scalar.copy(out=dst, in_=src)
                 a += share
-            quantize(grouped[:], codes[:, c0 : c0 + width], scales[:, c0 : c0 + width])
+            return grouped
 
-        def quantize(grouped, codes, scales):
+        def quantize(name, grouped, width):
+            codes = tile([P, width], U32, f"{name}_codes")
+            scales = tile([P, width], U8, f"{name}_scales")
             nc.vector.quantize_mx(
-                out=codes.bitcast(FP8X4), scales=scales, in_=grouped.rearrange("p w j -> p (w j)")
+                out=codes[:].bitcast(FP8X4), scales=scales[:], in_=grouped[:].rearrange("p w j -> p (w j)")
             )
+            return codes, scales
 
-        x_codes = keep.tile([P, T], U32, name="x_codes", align_bytes=64)
-        x_scales = keep.tile([P, T], U8, name="x_scales", align_bytes=64)
-        chunk_codes(x_raw, (T,), (0, T, (("v", 128),)), "x", x_codes, x_scales)
+        def round_all(name, raws, pieces):
+            rounded = []
+            c0 = 0
+            for copies in pieces:
+                width = sum(share for engine, share in copies)
+                rounded.append((c0, width, round_and_group(name, raws, c0, copies)))
+                c0 += width
+            return rounded
 
-        w1_codes = keep.tile([P, H], U32, name="w1_codes", align_bytes=64)
-        w1_scales = keep.tile([P, H], U8, name="w1_scales", align_bytes=64)
-        h = keep.tile([P, H], F32, name="h", align_bytes=64)
-        h16 = keep.tile([P, H], BF16, name="h16", align_bytes=64)
-        accs = []
-        for chunk in W1_CHUNKS:
-            c0, width, shares = chunk
-            cols = slice(c0, c0 + width)
-            chunk_codes(w1_raw, W1_LOADS, chunk, "w1", w1_codes, w1_scales)
-            acc = psum.tile([P, width], F32, name=f"acc{c0}")
-            accs.append((cols, acc))
+        def quantize_all(name, rounded):
+            return [(c0, width, quantize(f"{name}{c0}", grouped, width)) for c0, width, grouped in rounded]
+
+        x_rounded = round_all("x", x_raw, X_PIECES)
+        w1_rounded = round_all("w1", w1_raw, W1_PIECES)
+        x_codes, x_scales = quantize_all("x", x_rounded)[0][2]
+        h = tile([P, H], BF16, "h")
+        for i, (c0, width, (codes, scales)) in enumerate(quantize_all("w1", w1_rounded)):
+            acc = psum.tile([P, width], F32, name=f"acc{i}", tag=f"bank{i}")
             nc.tensor.matmul_mx(
                 out=acc[:],
                 lhsT=x_codes[:].bitcast(FP8X4),
                 lhsT_scale=x_scales[:],
-                rhs=w1_codes[:, cols].bitcast(FP8X4),
-                rhs_scale=w1_scales[:, cols],
+                rhs=codes[:].bitcast(FP8X4),
+                rhs_scale=scales[:],
                 start=True,
                 stop=True,
             )
-            nc.scalar.activation(h[:, cols], acc[:], SILU)
+            nc.scalar.activation(h[:, c0 : c0 + width], acc[:], SILU)
 
-        for cols, acc in accs:
-            nc.scalar.activation(h16[:, cols], acc[:], SILU)
-        picked = keep.tile([P, H], BF16, name="picked", align_bytes=64)
-        ordered = picked[:].rearrange("q (u p e) -> q p u e", u=2, e=2)
-        nc.vector.tensor_copy(
-            ordered[:, 0 : V_GATHER // PACK], h[:].indirect(offsets[:, 0 : V_GATHER // 16])
-        )
-        if V_GATHER < H:
-            nc.scalar.activation(
-                ordered[:, V_GATHER // PACK : P], h16[:].indirect(offsets[:, V_GATHER // 16 : H // 16]), COPY
-            )
+        picked = tile([P, H], BF16, "picked")
+        nc.vector.tensor_copy(picked[:, 0:V_GATHER], h[:].indirect(offsets[:, 0 : V_GATHER // 16]))
+        nc.scalar.activation(picked[:, V_GATHER:H], h[:].indirect(offsets[:, V_GATHER // 16 : H // 16]), COPY)
 
         turned = psum.tile([P, 2, T], F32, name="turned")
         words = picked[:].bitcast(F32)
         for u in range(2):
-            nc.tensor.transpose(turned[:, u, :], words[:, u * P : (u + 1) * P], ident[:])
-        h_grouped = keep.tile([P, T, PACK], BF16, name="h_grouped", align_bytes=64)
+            nc.tensor.transpose(turned[:, u, :], words[:, u : H // 2 : 2], ident[:])
+        h_grouped = tile([P, T, PACK], BF16, "h_grouped")
         nc.scalar.copy(
             out=h_grouped[:].rearrange("p t j -> p (t j)").bitcast(F32).rearrange("p (t u) -> p t u", u=2),
             in_=turned[:].rearrange("p u t -> p t u"),
         )
-        h_codes = keep.tile([P, T], U32, name="h_codes", align_bytes=64)
-        h_scales = keep.tile([P, T], U8, name="h_scales", align_bytes=64)
-        quantize(h_grouped[:], h_codes[:], h_scales[:])
+        h_codes, h_scales = quantize("h", h_grouped, T)
+        w2_codes = quantize_all("w2", round_all("w2", w2_raw, W2_PIECES))
 
-        w2_codes = keep.tile([P, N], U32, name="w2_codes", align_bytes=64)
-        w2_scales = keep.tile([P, N], U8, name="w2_scales", align_bytes=64)
-        for chunk in W2_CHUNKS:
-            chunk_codes(w2_raw, W2_LOADS, chunk, "w2", w2_codes, w2_scales)
-
-        blocks = N // P
-        results = keep.tile([P, blocks, T], F32, name="results")
-        for b in range(blocks):
-            m = slice(b * P, (b + 1) * P)
-            acc2 = psum.tile([P, T], F32, name=f"acc2_{b}", tag=BANKS[b])
-            nc.tensor.matmul_mx(
-                out=acc2[:],
-                lhsT=w2_codes[:, m].bitcast(FP8X4),
-                lhsT_scale=w2_scales[:, m],
-                rhs=h_codes[:].bitcast(FP8X4),
-                rhs_scale=h_scales[:],
-                start=True,
-                stop=True,
-            )
-            if b % 2 == 0:
-                nc.vector.tensor_copy(out=results[:, b, :], in_=acc2[:])
-            else:
-                nc.scalar.copy(out=results[:, b, :], in_=acc2[:])
+        results = keep.tile([P, N // P, T], F32, name="results")
+        for c0, width, (codes, scales) in w2_codes:
+            for a in range(0, width, P):
+                b = (c0 + a) // P
+                acc2 = psum.tile([P, T], F32, name=f"acc2_{b}", tag=f"bank{b}")
+                nc.tensor.matmul_mx(
+                    out=acc2[:],
+                    lhsT=codes[:, a : a + P].bitcast(FP8X4),
+                    lhsT_scale=scales[:, a : a + P],
+                    rhs=h_codes[:].bitcast(FP8X4),
+                    rhs_scale=h_scales[:],
+                    start=True,
+                    stop=True,
+                )
+                if b % 2 == 0:
+                    nc.vector.tensor_copy(out=results[:, b, :], in_=acc2[:])
+                else:
+                    nc.scalar.copy(out=results[:, b, :], in_=acc2[:])
         rows = out.rearrange("(b p) t -> p b t", p=P)
-        nc.sync.dma_start(rows[:, 0:2, :], results[:, 0:2, :])
-        nc.sync.dma_start(rows[:, 2:3, :], results[:, 2:3, :])
-        nc.scalar.dma_start(rows[:, 3:4, :], results[:, 3:4, :])
+        for b in range(N // P):
+            queue = nc.scalar if b == N // P - 1 else nc.sync
+            queue.dma_start(rows[:, b, :], results[:, b, :])

@@ -24,7 +24,7 @@ X_PIECES = ((("vector", 128),),)
 W1_LOADS = (128, 128, 128, 128)
 W1_PIECES = ((("scalar", 128),), (("vector", 128),), (("scalar", 128),), (("vector", 128),),)
 W2_LOADS = (128, 128, 256)
-W2_PIECES = ((("vector", 128),), (("gpsimd", 128),), (("vector", 160), ("scalar", 96),),)
+W2_PIECES = ((("vector", 128),), (("vector", 128),), (("vector", 128), ("scalar", 128),),)
 REUSED = {"w2256_grouped": 0, "h": 1536, "w2128_scales": 2048}
 V_GATHER = 256
 
@@ -41,9 +41,8 @@ def tile_picked_shuffle_mlp_silu_perm_l_kernel(tc, xT, w1, w2, offs, out):
                 return reuse.tile(shape, dtype, name=name, offset=REUSED[name], align_bytes=64)
             return keep.tile(shape, dtype, name=name, align_bytes=64)
 
-        def load(dram, widths, name):
+        def load(dram, widths, name, c0=0):
             raws = []
-            c0 = 0
             for width in widths:
                 raw = tile([P, PACK, width], F32, f"{name}_raw{c0}")
                 nc.sync.dma_start(raw[:], dram[:, c0 : c0 + width].rearrange("(p j) w -> p j w", j=PACK))
@@ -54,8 +53,9 @@ def tile_picked_shuffle_mlp_silu_perm_l_kernel(tc, xT, w1, w2, offs, out):
         offsets = keep.tile([P, H // 16], U16, name="offsets")
         x_raw = load(xT, X_LOADS, "x")
         w1_raw = load(w1, W1_LOADS, "w1")
+        w2_raw = load(w2, W2_LOADS[:2], "w2", 0)
         nc.sync.dma_start(offsets[:], offs)
-        w2_raw = load(w2, W2_LOADS, "w2")
+        w2_raw += load(w2, W2_LOADS[2:], "w2", sum(W2_LOADS[:2]))
 
         warm = keep.tile([P, 1], F32, name="warm")
         nc.vector.memset(warm[:], 0.0)
@@ -139,8 +139,8 @@ def tile_picked_shuffle_mlp_silu_perm_l_kernel(tc, xT, w1, w2, offs, out):
             out=h_grouped[:].rearrange("p t j -> p (t j)").bitcast(F32).rearrange("p (t u) -> p t u", u=2),
             in_=turned[:].rearrange("p u t -> p t u"),
         )
-        h_codes, h_scales = quantize("h", h_grouped, T)
         w2_codes = quantize_all("w2", round_all("w2", w2_raw, W2_PIECES))
+        h_codes, h_scales = quantize("h", h_grouped, T)
 
         results = keep.tile([P, N // P, T], F32, name="results")
         for c0, width, (codes, scales) in w2_codes:

@@ -21,11 +21,12 @@ LINE = 4
 
 X_LOADS = (128,)
 X_PIECES = ((("vector", 128),),)
-W1_LOADS = (128, 128, 128, 128)
-W1_PIECES = ((("scalar", 128),), (("vector", 128),), (("scalar", 128),), (("vector", 128),),)
-W2_LOADS = (128, 128, 256)
-W2_PIECES = ((("vector", 128),), (("vector", 128),), (("vector", 128), ("scalar", 128),),)
-REUSED = {"w2256_grouped": 0, "h": 1536, "w2128_scales": 2048}
+W1_LOADS = (256, 128, 128)
+W1_PIECES = ((("vector", 128),), (("vector", 32), ("scalar", 96),), (("scalar", 128),), (("vector", 64), ("vector", 64),),)
+W2_LOADS = (128, 128, 128, 128)
+W2_PIECES = ((("vector", 128),), (("vector", 128),), (("scalar", 128),), (("vector", 128),),)
+REUSED = {"w2256_grouped": 0, "h": 512, "w2128_scales": 1024, "w2384_grouped": 1280}
+HALVED = ("w1384",)
 V_GATHER = 256
 
 
@@ -92,9 +93,13 @@ def tile_picked_shuffle_mlp_silu_perm_l_kernel(tc, xT, w1, w2, offs, out):
         def quantize(name, grouped, width):
             codes = tile([P, width], U32, f"{name}_codes")
             scales = tile([P, width], U8, f"{name}_scales")
-            nc.vector.quantize_mx(
-                out=codes[:].bitcast(FP8X4), scales=scales[:], in_=grouped[:].rearrange("p w j -> p (w j)")
-            )
+            step = width // 2 if name in HALVED else width
+            for a in range(0, width, step):
+                nc.vector.quantize_mx(
+                    out=codes[:, a : a + step].bitcast(FP8X4),
+                    scales=scales[:, a : a + step],
+                    in_=grouped[:, a : a + step, :].rearrange("p w j -> p (w j)"),
+                )
             return codes, scales
 
         def round_all(name, raws, pieces):
@@ -135,12 +140,19 @@ def tile_picked_shuffle_mlp_silu_perm_l_kernel(tc, xT, w1, w2, offs, out):
         for u in range(2):
             nc.tensor.transpose(turned[:, u, :], words[:, u : H // 2 : 2], ident[:])
         h_grouped = tile([P, T, PACK], BF16, "h_grouped")
-        nc.scalar.copy(
-            out=h_grouped[:].rearrange("p t j -> p (t j)").bitcast(F32).rearrange("p (t u) -> p t u", u=2),
-            in_=turned[:].rearrange("p u t -> p t u"),
-        )
+        h_words = h_grouped[:].rearrange("p t j -> p (t j)").bitcast(F32).rearrange("p (t u) -> p t u", u=2)
+        halves = (slice(0, T // 2), slice(T // 2, T))
+        for tokens in halves:
+            nc.scalar.copy(out=h_words[:, tokens, :], in_=turned[:].rearrange("p u t -> p t u")[:, tokens, :])
         w2_codes = quantize_all("w2", round_all("w2", w2_raw, W2_PIECES))
-        h_codes, h_scales = quantize("h", h_grouped, T)
+        h_codes = tile([P, T], U32, "h_codes")
+        h_scales = tile([P, T], U8, "h_scales")
+        for tokens in halves:
+            nc.vector.quantize_mx(
+                out=h_codes[:, tokens].bitcast(FP8X4),
+                scales=h_scales[:, tokens],
+                in_=h_grouped[:, tokens, :].rearrange("p w j -> p (w j)"),
+            )
 
         results = keep.tile([P, N // P, T], F32, name="results")
         for c0, width, (codes, scales) in w2_codes:

@@ -25,7 +25,7 @@ W1_LOADS = (256, 128, 128)
 W1_PIECES = ((("vector", 128),), (("vector", 32), ("scalar", 96),), (("scalar", 128),), (("vector", 64), ("vector", 64),),)
 W2_LOADS = (128, 128, 128, 128)
 W2_PIECES = ((("vector", 128),), (("vector", 128),), (("scalar", 128),), (("vector", 128),),)
-REUSED = {"w2256_grouped": 0, "h": 512, "w2128_scales": 1024, "w2384_grouped": 1280}
+REUSED = {"w2256_grouped": 0, "h": 512, "w2128_scales": 1024, "w2384_grouped": 1280, "h_grouped0": 4096, "w2256_scales": 4096, "w2384_scales": 4224}
 HALVED = ("w1384",)
 V_GATHER = 256
 
@@ -139,20 +139,26 @@ def tile_picked_shuffle_mlp_silu_perm_l_kernel(tc, xT, w1, w2, offs, out):
         words = picked[:].bitcast(F32)
         for u in range(2):
             nc.tensor.transpose(turned[:, u, :], words[:, u : H // 2 : 2], ident[:])
-        h_grouped = tile([P, T, PACK], BF16, "h_grouped")
-        h_words = h_grouped[:].rearrange("p t j -> p (t j)").bitcast(F32).rearrange("p (t u) -> p t u", u=2)
         halves = (slice(0, T // 2), slice(T // 2, T))
-        for tokens in halves:
-            nc.scalar.copy(out=h_words[:, tokens, :], in_=turned[:].rearrange("p u t -> p t u")[:, tokens, :])
-        w2_codes = quantize_all("w2", round_all("w2", w2_raw, W2_PIECES))
+        h_grouped = []
+        for i, tokens in enumerate(halves):
+            grouped = tile([P, T // 2, PACK], BF16, f"h_grouped{i}")
+            nc.scalar.copy(
+                out=grouped[:].rearrange("p t j -> p (t j)").bitcast(F32).rearrange("p (t u) -> p t u", u=2),
+                in_=turned[:].rearrange("p u t -> p t u")[:, tokens, :],
+            )
+            h_grouped.append(grouped)
+        w2_rounded = round_all("w2", w2_raw, W2_PIECES)
+        w2_codes = quantize_all("w2", w2_rounded[:-2])
         h_codes = tile([P, T], U32, "h_codes")
         h_scales = tile([P, T], U8, "h_scales")
-        for tokens in halves:
+        for tokens, grouped in zip(halves, h_grouped):
             nc.vector.quantize_mx(
                 out=h_codes[:, tokens].bitcast(FP8X4),
                 scales=h_scales[:, tokens],
-                in_=h_grouped[:, tokens, :].rearrange("p w j -> p (w j)"),
+                in_=grouped[:].rearrange("p w j -> p (w j)"),
             )
+        w2_codes += quantize_all("w2", w2_rounded[-2:])
 
         results = keep.tile([P, N // P, T], F32, name="results")
         for c0, width, (codes, scales) in w2_codes:

@@ -25,8 +25,9 @@ W1_LOADS = (256, 128, 128)
 W1_PIECES = ((("vector", 128),), (("vector", 32), ("scalar", 96),), (("scalar", 128),), (("vector", 64), ("vector", 64),),)
 W2_LOADS = (128, 128, 128, 128)
 W2_PIECES = ((("vector", 128),), (("vector", 128),), (("scalar", 128),), (("vector", 128),),)
-REUSED = {"w2256_grouped": 0, "h": 512, "w2128_scales": 1024, "w2384_grouped": 1280, "h_grouped0": 4096, "w2256_scales": 4096, "w2384_scales": 4224}
+REUSED = {"w2256_grouped": 0, "h": 512, "w2128_scales": 1024, "w2384_grouped": 1280, "h_grouped0": 4096, "w2256_scales": 4096, "w2384_scales": 4224, "w2_raw384": 8192, "h_scales": 8192}
 HALVED = ("w1384",)
+BY_PAIRS = ("w2_raw256", "w2_raw384")
 V_GATHER = 256
 
 
@@ -46,7 +47,10 @@ def tile_picked_shuffle_mlp_silu_perm_l_kernel(tc, xT, w1, w2, offs, out):
             raws = []
             for width in widths:
                 raw = tile([P, PACK, width], F32, f"{name}_raw{c0}")
-                nc.sync.dma_start(raw[:], dram[:, c0 : c0 + width].rearrange("(p j) w -> p j w", j=PACK))
+                rows = dram[:, c0 : c0 + width].rearrange("(p j) w -> p j w", j=PACK)
+                step = 2 if f"{name}_raw{c0}" in BY_PAIRS else PACK
+                for j in range(0, PACK, step):
+                    nc.sync.dma_start(raw[:, j : j + step, :], rows[:, j : j + step, :])
                 raws.append((c0, width, raw))
                 c0 += width
             return raws

@@ -27,7 +27,7 @@ W2_LOADS = (128, 128, 128, 128)
 W2_PIECES = ((("vector", 128),), (("vector", 128),), (("scalar", 128),), (("vector", 128),),)
 REUSED = {"w2256_grouped": 0, "h": 512, "w2128_scales": 1024, "w2384_grouped": 1280, "h_grouped0": 4096, "w2256_scales": 4096, "w2384_scales": 4224, "w2_raw384": 8192, "h_scales": 8192}
 HALVED = ("w1384",)
-BY_PAIRS = ("w2_raw256", "w2_raw384")
+BY_PAIRS = ("w2_raw384",)
 V_GATHER = 256
 
 
@@ -48,7 +48,7 @@ def tile_picked_shuffle_mlp_silu_perm_l_kernel(tc, xT, w1, w2, offs, out):
             for width in widths:
                 raw = tile([P, PACK, width], F32, f"{name}_raw{c0}")
                 rows = dram[:, c0 : c0 + width].rearrange("(p j) w -> p j w", j=PACK)
-                step = 2 if f"{name}_raw{c0}" in BY_PAIRS else PACK
+                step = 1 if f"{name}_raw{c0}" in BY_PAIRS else PACK
                 for j in range(0, PACK, step):
                     nc.sync.dma_start(raw[:, j : j + step, :], rows[:, j : j + step, :])
                 raws.append((c0, width, raw))
@@ -183,6 +183,5 @@ def tile_picked_shuffle_mlp_silu_perm_l_kernel(tc, xT, w1, w2, offs, out):
                 else:
                     nc.scalar.copy(out=results[:, b, :], in_=acc2[:])
         rows = out.rearrange("(b p) t -> p b t", p=P)
-        for b in range(N // P):
-            queue = nc.scalar if b == N // P - 1 else nc.sync
-            queue.dma_start(rows[:, b, :], results[:, b, :])
+        for first, last in ((0, 2), (2, 3), (3, 4)):
+            nc.sync.dma_start(rows[:, first:last, :], results[:, first:last, :])

@@ -22,12 +22,13 @@ LINE = 4
 X_LOADS = (128,)
 X_PIECES = ((("vector", 128),),)
 W1_LOADS = (256, 128, 128)
-W1_PIECES = ((("vector", 128),), (("vector", 32), ("scalar", 96),), (("scalar", 128),), (("vector", 64), ("vector", 64),),)
-W2_LOADS = (128, 128, 128, 128)
-W2_PIECES = ((("vector", 128),), (("vector", 128),), (("scalar", 128),), (("vector", 128),),)
-REUSED = {"w2256_grouped": 0, "h": 512, "w2128_scales": 1024, "w2384_grouped": 1280, "h_grouped0": 4096, "w2256_scales": 4096, "w2384_scales": 4224, "w2_raw384": 8192, "h_scales": 8192}
-HALVED = ("w1384",)
-BY_PAIRS = ("w2_raw384",)
+W1_PIECES = ((("vector", 128),), (("vector", 32), ("scalar", 96),), (("scalar", 128),), (("vector", 64),), (("vector", 64),),)
+W2_LOADS = (128, 256, 128)
+W2_PIECES = ((("vector", 128),), (("scalar", 128),), (("vector", 128),), (("vector", 128),),)
+REUSED = {"w2128_grouped": 0, "h": 512, "w2_late_grouped": 1280, "h_grouped0": 4096, "w2256_scales": 4096, "w2384_scales": 4224, "w2_raw384": 8192, "h_scales": 8192, "w2128_scales": 8320}
+LATE = ("w2256", "w2384")
+HALVED = ()
+ROWS_A_DMA = {"w2_raw128": 2, "w2_raw384": 1}
 V_GATHER = 256
 
 
@@ -48,7 +49,7 @@ def tile_picked_shuffle_mlp_silu_perm_l_kernel(tc, xT, w1, w2, offs, out):
             for width in widths:
                 raw = tile([P, PACK, width], F32, f"{name}_raw{c0}")
                 rows = dram[:, c0 : c0 + width].rearrange("(p j) w -> p j w", j=PACK)
-                step = 1 if f"{name}_raw{c0}" in BY_PAIRS else PACK
+                step = ROWS_A_DMA.get(f"{name}_raw{c0}", PACK)
                 for j in range(0, PACK, step):
                     nc.sync.dma_start(raw[:, j : j + step, :], rows[:, j : j + step, :])
                 raws.append((c0, width, raw))
@@ -58,9 +59,9 @@ def tile_picked_shuffle_mlp_silu_perm_l_kernel(tc, xT, w1, w2, offs, out):
         offsets = keep.tile([P, H // 16], U16, name="offsets")
         x_raw = load(xT, X_LOADS, "x")
         w1_raw = load(w1, W1_LOADS, "w1")
-        w2_raw = load(w2, W2_LOADS[:2], "w2", 0)
+        w2_raw = load(w2, W2_LOADS[:1], "w2", 0)
         nc.sync.dma_start(offsets[:], offs)
-        w2_raw += load(w2, W2_LOADS[2:], "w2", sum(W2_LOADS[:2]))
+        w2_raw += load(w2, W2_LOADS[1:], "w2", sum(W2_LOADS[:1]))
 
         warm = keep.tile([P, 1], F32, name="warm")
         nc.vector.memset(warm[:], 0.0)
@@ -68,8 +69,15 @@ def tile_picked_shuffle_mlp_silu_perm_l_kernel(tc, xT, w1, w2, offs, out):
         ident = keep.tile([P, P], F32, name="ident")
         make_identity(nc, ident[:])
 
+        late = []
+
         def round_and_group(name, raws, c0, copies):
-            grouped = tile([P, sum(share for engine, share in copies), PACK], BF16, f"{name}{c0}_grouped")
+            if f"{name}{c0}" in LATE:
+                if not late:
+                    late.append(tile([P, len(LATE), P, PACK], BF16, "w2_late_grouped"))
+                grouped = late[0][:, LATE.index(f"{name}{c0}")]
+            else:
+                grouped = tile([P, sum(share for engine, share in copies), PACK], BF16, f"{name}{c0}_grouped")
             a = 0
             for engine, share in copies:
                 first, width, raw = [r for r in raws if r[0] <= c0 + a < r[0] + r[1]][0]

@@ -20,15 +20,15 @@ PACK = 4
 LINE = 4
 
 X_LOADS = (128,)
-X_PIECES = ((("vector", 128),),)
-W1_LOADS = (256, 128, 128)
-W1_PIECES = ((("vector", 128),), (("vector", 32), ("scalar", 96),), (("scalar", 128),), (("vector", 64),), (("vector", 64),),)
-W2_LOADS = (128, 256, 128)
+X_PIECES = ((("vector", 64), ("scalar", 64),),)
+W1_LOADS = (384, 128)
+W1_PIECES = ((("vector", 128),), (("scalar", 128),), (("vector", 128),), (("vector", 64),), (("vector", 64),),)
+W2_LOADS = (128, 384)
 W2_PIECES = ((("vector", 128),), (("scalar", 128),), (("vector", 128),), (("vector", 128),),)
-REUSED = {"w2128_grouped": 0, "h": 512, "w2_late_grouped": 1280, "h_grouped0": 4096, "w2256_scales": 4096, "w2384_scales": 4224, "w2_raw384": 8192, "h_scales": 8192, "w2128_scales": 8320}
+REUSED = {"w2128_grouped": 0, "h": 512, "w2_late_grouped": 1280, "h_grouped0": 4096, "w2256_scales": 4096, "w2384_scales": 4224, "w2_raw128": 8192, "h_scales": 8192}
 LATE = ("w2256", "w2384")
 HALVED = ()
-ROWS_A_DMA = {"w2_raw128": 2, "w2_raw384": 1}
+ROWS_A_DMA = {}
 V_GATHER = 256
 
 
@@ -57,8 +57,9 @@ def tile_picked_shuffle_mlp_silu_perm_l_kernel(tc, xT, w1, w2, offs, out):
             return raws
 
         offsets = keep.tile([P, H // 16], U16, name="offsets")
+        w1_raw = load(w1, W1_LOADS[:1], "w1")
         x_raw = load(xT, X_LOADS, "x")
-        w1_raw = load(w1, W1_LOADS, "w1")
+        w1_raw += load(w1, W1_LOADS[1:], "w1", W1_LOADS[0])
         w2_raw = load(w2, W2_LOADS[:1], "w2", 0)
         nc.sync.dma_start(offsets[:], offs)
         w2_raw += load(w2, W2_LOADS[1:], "w2", sum(W2_LOADS[:1]))
@@ -191,5 +192,5 @@ def tile_picked_shuffle_mlp_silu_perm_l_kernel(tc, xT, w1, w2, offs, out):
                 else:
                     nc.scalar.copy(out=results[:, b, :], in_=acc2[:])
         rows = out.rearrange("(b p) t -> p b t", p=P)
-        for first, last in ((0, 2), (2, 3), (3, 4)):
+        for first, last in ((0, 2), (2, 4)):
             nc.sync.dma_start(rows[:, first:last, :], results[:, first:last, :])

@@ -23,10 +23,10 @@ X_LOADS = (128,)
 X_PIECES = ((("vector", 64), ("scalar", 64),),)
 W1_LOADS = (384, 128)
 W1_PIECES = ((("vector", 128),), (("scalar", 128),), (("vector", 128),), (("vector", 64),), (("vector", 64),),)
-W2_LOADS = (128, 384)
-W2_PIECES = ((("vector", 128),), (("scalar", 128),), (("vector", 128),), (("vector", 128),),)
-REUSED = {"w2128_grouped": 0, "h": 512, "w2_late_grouped": 1280, "h_grouped0": 4096, "w2256_scales": 4096, "w2384_scales": 4224, "w2_raw128": 8192, "h_scales": 8192}
-LATE = ("w2256", "w2384")
+W2_LOADS = (512,)
+W2_PIECES = ((("vector", 128),), (("vector", 128),), (("vector", 96), ("scalar", 32),), (("scalar", 128),),)
+REUSED = {"h_grouped0": 0, "w2128_scales": 0, "w2256_scales": 128, "w2384_scales": 256, "w2_raw0": 1024, "h_scales": 1024}
+LATE = ()
 HALVED = ()
 ROWS_A_DMA = {}
 V_GATHER = 256
@@ -60,9 +60,8 @@ def tile_picked_shuffle_mlp_silu_perm_l_kernel(tc, xT, w1, w2, offs, out):
         w1_raw = load(w1, W1_LOADS[:1], "w1")
         x_raw = load(xT, X_LOADS, "x")
         w1_raw += load(w1, W1_LOADS[1:], "w1", W1_LOADS[0])
-        w2_raw = load(w2, W2_LOADS[:1], "w2", 0)
         nc.sync.dma_start(offsets[:], offs)
-        w2_raw += load(w2, W2_LOADS[1:], "w2", sum(W2_LOADS[:1]))
+        w2_raw = load(w2, W2_LOADS, "w2")
 
         warm = keep.tile([P, 1], F32, name="warm")
         nc.vector.memset(warm[:], 0.0)
@@ -162,7 +161,7 @@ def tile_picked_shuffle_mlp_silu_perm_l_kernel(tc, xT, w1, w2, offs, out):
             )
             h_grouped.append(grouped)
         w2_rounded = round_all("w2", w2_raw, W2_PIECES)
-        w2_codes = quantize_all("w2", w2_rounded[:-2])
+        w2_codes = quantize_all("w2", w2_rounded[:1])
         h_codes = tile([P, T], U32, "h_codes")
         h_scales = tile([P, T], U8, "h_scales")
         for tokens, grouped in zip(halves, h_grouped):
@@ -171,7 +170,7 @@ def tile_picked_shuffle_mlp_silu_perm_l_kernel(tc, xT, w1, w2, offs, out):
                 scales=h_scales[:, tokens],
                 in_=grouped[:].rearrange("p w j -> p (w j)"),
             )
-        w2_codes += quantize_all("w2", w2_rounded[-2:])
+        w2_codes += quantize_all("w2", w2_rounded[1:])
 
         results = keep.tile([P, N // P, T], F32, name="results")
         for c0, width, (codes, scales) in w2_codes:
@@ -192,5 +191,5 @@ def tile_picked_shuffle_mlp_silu_perm_l_kernel(tc, xT, w1, w2, offs, out):
                 else:
                     nc.scalar.copy(out=results[:, b, :], in_=acc2[:])
         rows = out.rearrange("(b p) t -> p b t", p=P)
-        for first, last in ((0, 2), (2, 4)):
+        for first, last in ((0, 2), (2, 3), (3, 4)):
             nc.sync.dma_start(rows[:, first:last, :], results[:, first:last, :])

@@ -21,15 +21,15 @@ LINE = 4
 
 X_LOADS = (128,)
 X_PIECES = ((("vector", 64), ("scalar", 64),),)
-W1_LOADS = (384, 128)
-W1_PIECES = ((("vector", 128),), (("scalar", 128),), (("vector", 128),), (("vector", 64),), (("vector", 64),),)
+W1_LOADS = (320, 192)
+W1_PIECES = ((("vector", 128),), (("scalar", 128),), (("vector", 64),), (("vector", 64),), (("scalar", 64),), (("vector", 64),),)
 W2_LOADS = (512,)
 W2_PIECES = ((("vector", 128),), (("vector", 128),), (("vector", 96), ("scalar", 32),), (("scalar", 128),),)
 REUSED = {"h_grouped0": 0, "w2128_scales": 0, "w2256_scales": 128, "w2384_scales": 256, "w2_raw0": 1024, "h_scales": 1024}
 LATE = ()
 HALVED = ()
 ROWS_A_DMA = {}
-V_GATHER = 256
+V_GATHER = 288
 
 
 def tile_picked_shuffle_mlp_silu_perm_l_kernel(tc, xT, w1, w2, offs, out):

@@ -18,17 +18,12 @@ COPY = mybir.ActivationFunctionType.Copy
 P = 128
 PACK = 4
 LINE = 4
+PAIR = 2
 
-X_LOADS = (128,)
-X_PIECES = ((("vector", 64), ("scalar", 64),),)
-W1_LOADS = (320, 192)
-W1_PIECES = ((("vector", 128),), (("scalar", 128),), (("vector", 64),), (("vector", 64),), (("scalar", 64),), (("vector", 64),),)
-W2_LOADS = (512,)
-W2_PIECES = ((("vector", 128),), (("vector", 128),), (("vector", 96), ("scalar", 32),), (("scalar", 128),),)
-REUSED = {"h_grouped0": 0, "w2128_scales": 0, "w2256_scales": 128, "w2384_scales": 256, "w2_raw0": 1024, "h_scales": 1024}
-LATE = ()
-HALVED = ()
-ROWS_A_DMA = {}
+W1_EARLY = 320
+W1_PIECES = (("vector", 128), ("scalar", 128), ("vector", 64), ("vector", 64), ("vector", 64), ("scalar", 64))
+X_ON_VECTOR = 64
+W2_ON_SCALAR = 160
 V_GATHER = 288
 
 
@@ -39,29 +34,54 @@ def tile_picked_shuffle_mlp_silu_perm_l_kernel(tc, xT, w1, w2, offs, out):
         reuse = ctx.enter_context(tc.tile_pool(name="reuse", bufs=1))
         psum = ctx.enter_context(tc.psum_pool(name="psum", bufs=1))
 
-        def tile(shape, dtype, name):
-            if name in REUSED:
-                return reuse.tile(shape, dtype, name=name, offset=REUSED[name], align_bytes=64)
+        def kept(shape, dtype, name):
             return keep.tile(shape, dtype, name=name, align_bytes=64)
 
-        def load(dram, widths, name, c0=0):
-            raws = []
-            for width in widths:
-                raw = tile([P, PACK, width], F32, f"{name}_raw{c0}")
-                rows = dram[:, c0 : c0 + width].rearrange("(p j) w -> p j w", j=PACK)
-                step = ROWS_A_DMA.get(f"{name}_raw{c0}", PACK)
-                for j in range(0, PACK, step):
-                    nc.sync.dma_start(raw[:, j : j + step, :], rows[:, j : j + step, :])
-                raws.append((c0, width, raw))
-                c0 += width
-            return raws
+        def placed(shape, dtype, name, offset):
+            return reuse.tile(shape, dtype, name=name, offset=offset, align_bytes=64)
 
+        def load(raw, dram):
+            nc.sync.dma_start(raw[:], dram.rearrange("(p j) w -> p j w", j=PACK))
+
+        def copy_on(engine, dst, src):
+            if engine == "vector":
+                nc.vector.tensor_copy(out=dst, in_=src)
+            else:
+                nc.scalar.copy(out=dst, in_=src)
+
+        def round_columns(engine, grouped, raw):
+            copy_on(
+                engine,
+                grouped.rearrange("p (c i) j -> p c j i", i=LINE),
+                raw.rearrange("p j (c i) -> p c j i", i=LINE),
+            )
+
+        def quantize(codes, scales, grouped):
+            nc.vector.quantize_mx(out=codes.bitcast(FP8X4), scales=scales, in_=grouped.rearrange("p w j -> p (w j)"))
+
+        def product(acc, stationary, moving):
+            nc.tensor.matmul_mx(
+                out=acc,
+                lhsT=stationary[0].bitcast(FP8X4),
+                lhsT_scale=stationary[1],
+                rhs=moving[0].bitcast(FP8X4),
+                rhs_scale=moving[1],
+                start=True,
+                stop=True,
+            )
+
+        H_GROUPED_AT, W2_RAW_AT = 0, 1024
+
+        w1_early = kept([P, PACK, W1_EARLY], F32, "w1_early")
+        x_raw = kept([P, PACK, T], F32, "x_raw")
+        w1_late = kept([P, PACK, H - W1_EARLY], F32, "w1_late")
         offsets = keep.tile([P, H // 16], U16, name="offsets")
-        w1_raw = load(w1, W1_LOADS[:1], "w1")
-        x_raw = load(xT, X_LOADS, "x")
-        w1_raw += load(w1, W1_LOADS[1:], "w1", W1_LOADS[0])
+        w2_raw = placed([P, PACK, N], F32, "w2_raw", W2_RAW_AT)
+        load(w1_early, w1[:, 0:W1_EARLY])
+        load(x_raw, xT)
+        load(w1_late, w1[:, W1_EARLY:H])
         nc.sync.dma_start(offsets[:], offs)
-        w2_raw = load(w2, W2_LOADS, "w2")
+        load(w2_raw, w2)
 
         warm = keep.tile([P, 1], F32, name="warm")
         nc.vector.memset(warm[:], 0.0)
@@ -69,81 +89,38 @@ def tile_picked_shuffle_mlp_silu_perm_l_kernel(tc, xT, w1, w2, offs, out):
         ident = keep.tile([P, P], F32, name="ident")
         make_identity(nc, ident[:])
 
-        late = []
-
-        def round_and_group(name, raws, c0, copies):
-            if f"{name}{c0}" in LATE:
-                if not late:
-                    late.append(tile([P, len(LATE), P, PACK], BF16, "w2_late_grouped"))
-                grouped = late[0][:, LATE.index(f"{name}{c0}")]
+        x_grouped = kept([P, T, PACK], BF16, "x_grouped")
+        round_columns("vector", x_grouped[:, 0:X_ON_VECTOR, :], x_raw[:, :, 0:X_ON_VECTOR])
+        round_columns("scalar", x_grouped[:, X_ON_VECTOR:T, :], x_raw[:, :, X_ON_VECTOR:T])
+        w1_grouped = []
+        c0 = 0
+        for engine, width in W1_PIECES:
+            grouped = kept([P, width, PACK], BF16, f"w1_grouped{c0}")
+            if c0 < W1_EARLY:
+                raw = w1_early[:, :, c0 : c0 + width]
             else:
-                grouped = tile([P, sum(share for engine, share in copies), PACK], BF16, f"{name}{c0}_grouped")
-            a = 0
-            for engine, share in copies:
-                first, width, raw = [r for r in raws if r[0] <= c0 + a < r[0] + r[1]][0]
-                dst = grouped[:, a : a + share, :]
-                src = raw[:, :, c0 + a - first : c0 + a - first + share]
-                if engine == "gpsimd":
-                    nc.gpsimd.tensor_scalar(
-                        out=dst,
-                        in0=src.rearrange("p j w -> p w j"),
-                        scalar1=1.0,
-                        scalar2=0.0,
-                        op0=mybir.AluOpType.mult,
-                        op1=mybir.AluOpType.add,
-                    )
-                else:
-                    dst = dst.rearrange("p (c i) j -> p c j i", i=LINE)
-                    src = src.rearrange("p j (c i) -> p c j i", i=LINE)
-                    if engine == "vector":
-                        nc.vector.tensor_copy(out=dst, in_=src)
-                    else:
-                        nc.scalar.copy(out=dst, in_=src)
-                a += share
-            return grouped
+                raw = w1_late[:, :, c0 - W1_EARLY : c0 - W1_EARLY + width]
+            round_columns(engine, grouped[:], raw)
+            w1_grouped.append((c0, width, grouped))
+            c0 += width
 
-        def quantize(name, grouped, width):
-            codes = tile([P, width], U32, f"{name}_codes")
-            scales = tile([P, width], U8, f"{name}_scales")
-            step = width // 2 if name in HALVED else width
-            for a in range(0, width, step):
-                nc.vector.quantize_mx(
-                    out=codes[:, a : a + step].bitcast(FP8X4),
-                    scales=scales[:, a : a + step],
-                    in_=grouped[:, a : a + step, :].rearrange("p w j -> p (w j)"),
-                )
-            return codes, scales
+        x_codes = kept([P, T], U32, "x_codes")
+        x_scales = kept([P, T], U8, "x_scales")
+        quantize(x_codes[:], x_scales[:], x_grouped[:])
+        w1_mx = []
+        for c0, width, grouped in w1_grouped:
+            codes = kept([P, width], U32, f"w1_codes{c0}")
+            scales = kept([P, width], U8, f"w1_scales{c0}")
+            quantize(codes[:], scales[:], grouped[:])
+            w1_mx.append((c0, width, codes, scales))
 
-        def round_all(name, raws, pieces):
-            rounded = []
-            c0 = 0
-            for copies in pieces:
-                width = sum(share for engine, share in copies)
-                rounded.append((c0, width, round_and_group(name, raws, c0, copies)))
-                c0 += width
-            return rounded
-
-        def quantize_all(name, rounded):
-            return [(c0, width, quantize(f"{name}{c0}", grouped, width)) for c0, width, grouped in rounded]
-
-        x_rounded = round_all("x", x_raw, X_PIECES)
-        w1_rounded = round_all("w1", w1_raw, W1_PIECES)
-        x_codes, x_scales = quantize_all("x", x_rounded)[0][2]
-        h = tile([P, H], BF16, "h")
-        for i, (c0, width, (codes, scales)) in enumerate(quantize_all("w1", w1_rounded)):
+        h = kept([P, H], BF16, "h")
+        for i, (c0, width, codes, scales) in enumerate(w1_mx):
             acc = psum.tile([P, width], F32, name=f"acc{i}", tag=f"bank{i}")
-            nc.tensor.matmul_mx(
-                out=acc[:],
-                lhsT=x_codes[:].bitcast(FP8X4),
-                lhsT_scale=x_scales[:],
-                rhs=codes[:].bitcast(FP8X4),
-                rhs_scale=scales[:],
-                start=True,
-                stop=True,
-            )
+            product(acc[:], (x_codes[:], x_scales[:]), (codes[:], scales[:]))
             nc.scalar.activation(h[:, c0 : c0 + width], acc[:], SILU)
 
-        picked = tile([P, H], BF16, "picked")
+        picked = kept([P, H], BF16, "picked")
         nc.vector.tensor_copy(picked[:, 0:V_GATHER], h[:].indirect(offsets[:, 0 : V_GATHER // 16]))
         nc.scalar.activation(picked[:, V_GATHER:H], h[:].indirect(offsets[:, V_GATHER // 16 : H // 16]), COPY)
 
@@ -152,44 +129,41 @@ def tile_picked_shuffle_mlp_silu_perm_l_kernel(tc, xT, w1, w2, offs, out):
         for u in range(2):
             nc.tensor.transpose(turned[:, u, :], words[:, u : H // 2 : 2], ident[:])
         halves = (slice(0, T // 2), slice(T // 2, T))
-        h_grouped = []
-        for i, tokens in enumerate(halves):
-            grouped = tile([P, T // 2, PACK], BF16, f"h_grouped{i}")
+        h_grouped = [placed([P, T // 2, PACK], BF16, "h_grouped0", H_GROUPED_AT), kept([P, T // 2, PACK], BF16, "h_grouped1")]
+        for tokens, grouped in zip(halves, h_grouped):
             nc.scalar.copy(
                 out=grouped[:].rearrange("p t j -> p (t j)").bitcast(F32).rearrange("p (t u) -> p t u", u=2),
                 in_=turned[:].rearrange("p u t -> p t u")[:, tokens, :],
             )
-            h_grouped.append(grouped)
-        w2_rounded = round_all("w2", w2_raw, W2_PIECES)
-        w2_codes = quantize_all("w2", w2_rounded[:1])
-        h_codes = tile([P, T], U32, "h_codes")
-        h_scales = tile([P, T], U8, "h_scales")
-        for tokens, grouped in zip(halves, h_grouped):
-            nc.vector.quantize_mx(
-                out=h_codes[:, tokens].bitcast(FP8X4),
-                scales=h_scales[:, tokens],
-                in_=grouped[:].rearrange("p w j -> p (w j)"),
+
+        w2_grouped = [kept([P, PAIR, P, PACK], BF16, f"w2_grouped{g}") for g in range(N // (PAIR * P))]
+        for engine, first, last in (("vector", 0, PAIR * P), ("vector", PAIR * P, N - W2_ON_SCALAR), ("scalar", N - W2_ON_SCALAR, N)):
+            g, c0 = divmod(first, PAIR * P)
+            width = last - first
+            copy_on(
+                engine,
+                w2_grouped[g][:, :, c0 // PAIR : (c0 + width) // PAIR, :].rearrange("p e (c i) j -> p c j i e", i=LINE // PAIR),
+                w2_raw[:, :, first:last].rearrange("p j (c i e) -> p c j i e", i=LINE // PAIR, e=PAIR),
             )
-        w2_codes += quantize_all("w2", w2_rounded[1:])
+
+        def quantize_w2(b, scales):
+            codes = kept([P, P], U32, f"w2_codes{b}")
+            quantize(codes[:], scales[:], w2_grouped[b // PAIR][:, b % PAIR])
+            return codes[:], scales[:]
+
+        w2_mx = [quantize_w2(0, kept([P, P], U8, "w2_scales0"))]
+        h_codes = kept([P, T], U32, "h_codes")
+        h_scales = placed([P, T], U8, "h_scales", W2_RAW_AT)
+        for tokens, grouped in zip(halves, h_grouped):
+            quantize(h_codes[:, tokens], h_scales[:, tokens], grouped[:])
+        for b in range(1, N // P):
+            w2_mx.append(quantize_w2(b, placed([P, P], U8, f"w2_scales{b}", H_GROUPED_AT + (b - 1) * P)))
 
         results = keep.tile([P, N // P, T], F32, name="results")
-        for c0, width, (codes, scales) in w2_codes:
-            for a in range(0, width, P):
-                b = (c0 + a) // P
-                acc2 = psum.tile([P, T], F32, name=f"acc2_{b}", tag=f"bank{b}")
-                nc.tensor.matmul_mx(
-                    out=acc2[:],
-                    lhsT=codes[:, a : a + P].bitcast(FP8X4),
-                    lhsT_scale=scales[:, a : a + P],
-                    rhs=h_codes[:].bitcast(FP8X4),
-                    rhs_scale=h_scales[:],
-                    start=True,
-                    stop=True,
-                )
-                if b % 2 == 0:
-                    nc.vector.tensor_copy(out=results[:, b, :], in_=acc2[:])
-                else:
-                    nc.scalar.copy(out=results[:, b, :], in_=acc2[:])
-        rows = out.rearrange("(b p) t -> p b t", p=P)
-        for first, last in ((0, 2), (2, 3), (3, 4)):
-            nc.sync.dma_start(rows[:, first:last, :], results[:, first:last, :])
+        for b, weights in enumerate(w2_mx):
+            acc = psum.tile([P, T], F32, name=f"out_acc{b}", tag=f"bank{b}")
+            product(acc[:], weights, (h_codes[:], h_scales[:]))
+            copy_on("vector" if b % 2 == 0 else "scalar", results[:, b, :], acc[:])
+        rows = out.rearrange("(g p e) t -> p g e t", p=P, e=PAIR)
+        for g in range(N // (PAIR * P)):
+            nc.sync.dma_start(rows[:, g], results[:, PAIR * g : PAIR * (g + 1), :])

@@ -18,12 +18,11 @@ COPY = mybir.ActivationFunctionType.Copy
 P = 128
 PACK = 4
 LINE = 4
-PAIR = 2
+HALF = P // 2
 
 W1_EARLY = 320
-W1_PIECES = (("vector", 128), ("scalar", 128), ("vector", 64), ("vector", 64), ("vector", 64), ("scalar", 64))
+W1_PIECES = (("vector", 128), ("scalar", 128), ("vector", 64), ("vector", 64), ("scalar", 64), ("vector", 64))
 X_ON_VECTOR = 64
-W2_ON_SCALAR = 160
 V_GATHER = 288
 
 
@@ -70,13 +69,13 @@ def tile_picked_shuffle_mlp_silu_perm_l_kernel(tc, xT, w1, w2, offs, out):
                 stop=True,
             )
 
-        H_GROUPED_AT, W2_RAW_AT = 0, 1024
+        H_GROUPED_AT, PICKED_AT = 0, 1024
 
         w1_early = kept([P, PACK, W1_EARLY], F32, "w1_early")
         x_raw = kept([P, PACK, T], F32, "x_raw")
         w1_late = kept([P, PACK, H - W1_EARLY], F32, "w1_late")
         offsets = keep.tile([P, H // 16], U16, name="offsets")
-        w2_raw = placed([P, PACK, N], F32, "w2_raw", W2_RAW_AT)
+        w2_raw = kept([P, PACK, N], F32, "w2_raw")
         load(w1_early, w1[:, 0:W1_EARLY])
         load(x_raw, xT)
         load(w1_late, w1[:, W1_EARLY:H])
@@ -120,7 +119,7 @@ def tile_picked_shuffle_mlp_silu_perm_l_kernel(tc, xT, w1, w2, offs, out):
             product(acc[:], (x_codes[:], x_scales[:]), (codes[:], scales[:]))
             nc.scalar.activation(h[:, c0 : c0 + width], acc[:], SILU)
 
-        picked = kept([P, H], BF16, "picked")
+        picked = placed([P, H], BF16, "picked", PICKED_AT)
         nc.vector.tensor_copy(picked[:, 0:V_GATHER], h[:].indirect(offsets[:, 0 : V_GATHER // 16]))
         nc.scalar.activation(picked[:, V_GATHER:H], h[:].indirect(offsets[:, V_GATHER // 16 : H // 16]), COPY)
 
@@ -136,34 +135,36 @@ def tile_picked_shuffle_mlp_silu_perm_l_kernel(tc, xT, w1, w2, offs, out):
                 in_=turned[:].rearrange("p u t -> p t u")[:, tokens, :],
             )
 
-        w2_grouped = [kept([P, PAIR, P, PACK], BF16, f"w2_grouped{g}") for g in range(N // (PAIR * P))]
-        for engine, first, last in (("vector", 0, PAIR * P), ("vector", PAIR * P, N - W2_ON_SCALAR), ("scalar", N - W2_ON_SCALAR, N)):
-            g, c0 = divmod(first, PAIR * P)
-            width = last - first
-            copy_on(
-                engine,
-                w2_grouped[g][:, :, c0 // PAIR : (c0 + width) // PAIR, :].rearrange("p e (c i) j -> p c j i e", i=LINE // PAIR),
-                w2_raw[:, :, first:last].rearrange("p j (c i e) -> p c j i e", i=LINE // PAIR, e=PAIR),
-            )
+        w2_grouped = [kept([P, P, PACK], BF16, f"w2_grouped{b}") for b in range(3)]
+        last_halves = [kept([P, HALF, PACK], BF16, "w2_grouped3a"), placed([P, HALF, PACK], BF16, "w2_grouped3b", PICKED_AT)]
+        round_columns("vector", w2_grouped[0][:], w2_raw[:, :, 0:P])
+        round_columns("vector", w2_grouped[1][:], w2_raw[:, :, P : 2 * P])
+        round_columns("vector", w2_grouped[2][:, 0:HALF, :], w2_raw[:, :, 2 * P : 2 * P + HALF])
+        round_columns("scalar", w2_grouped[2][:, HALF:P, :], w2_raw[:, :, 2 * P + HALF : 3 * P])
+        round_columns("scalar", last_halves[0][:], w2_raw[:, :, 3 * P : 3 * P + HALF])
+        round_columns("scalar", last_halves[1][:], w2_raw[:, :, 3 * P + HALF : N])
 
-        def quantize_w2(b, scales):
+        def quantize_w2(b, scales, parts):
             codes = kept([P, P], U32, f"w2_codes{b}")
-            quantize(codes[:], scales[:], w2_grouped[b // PAIR][:, b % PAIR])
+            width = P // len(parts)
+            for i, grouped in enumerate(parts):
+                columns = slice(i * width, (i + 1) * width)
+                quantize(codes[:, columns], scales[:, columns], grouped[:])
             return codes[:], scales[:]
 
-        w2_mx = [quantize_w2(0, kept([P, P], U8, "w2_scales0"))]
+        w2_mx = [quantize_w2(0, kept([P, P], U8, "w2_scales0"), w2_grouped[0:1])]
         h_codes = kept([P, T], U32, "h_codes")
-        h_scales = placed([P, T], U8, "h_scales", W2_RAW_AT)
+        h_scales = kept([P, T], U8, "h_scales")
         for tokens, grouped in zip(halves, h_grouped):
             quantize(h_codes[:, tokens], h_scales[:, tokens], grouped[:])
-        for b in range(1, N // P):
-            w2_mx.append(quantize_w2(b, placed([P, P], U8, f"w2_scales{b}", H_GROUPED_AT + (b - 1) * P)))
+        for b, parts in ((1, w2_grouped[1:2]), (2, w2_grouped[2:3]), (3, last_halves)):
+            w2_mx.append(quantize_w2(b, placed([P, P], U8, f"w2_scales{b}", H_GROUPED_AT + (b - 1) * P), parts))
 
         results = keep.tile([P, N // P, T], F32, name="results")
         for b, weights in enumerate(w2_mx):
             acc = psum.tile([P, T], F32, name=f"out_acc{b}", tag=f"bank{b}")
             product(acc[:], weights, (h_codes[:], h_scales[:]))
             copy_on("vector" if b % 2 == 0 else "scalar", results[:, b, :], acc[:])
-        rows = out.rearrange("(g p e) t -> p g e t", p=P, e=PAIR)
-        for g in range(N // (PAIR * P)):
-            nc.sync.dma_start(rows[:, g], results[:, PAIR * g : PAIR * (g + 1), :])
+        rows = out.rearrange("(b p) t -> p b t", p=P)
+        for first, last in ((0, 2), (2, 3), (3, 4)):
+            nc.sync.dma_start(rows[:, first:last, :], results[:, first:last, :])

@@ -39,6 +39,9 @@ def tile_picked_shuffle_mlp_silu_perm_l_kernel(tc, xT, w1, w2, offs, out):
         def placed(shape, dtype, name, offset):
             return reuse.tile(shape, dtype, name=name, offset=offset, align_bytes=64)
 
+        def staged(shape, name):
+            return keep.tile(shape, F32, name=name, align_bytes=256)
+
         def load(raw, dram):
             nc.sync.dma_start(raw[:], dram.rearrange("(p j) w -> p j w", j=PACK))
 
@@ -71,11 +74,11 @@ def tile_picked_shuffle_mlp_silu_perm_l_kernel(tc, xT, w1, w2, offs, out):
 
         H_GROUPED_AT, PICKED_AT = 0, 1024
 
-        w1_early = kept([P, PACK, W1_EARLY], F32, "w1_early")
-        x_raw = kept([P, PACK, T], F32, "x_raw")
-        w1_late = kept([P, PACK, H - W1_EARLY], F32, "w1_late")
+        w1_early = staged([P, PACK, W1_EARLY], "w1_early")
+        x_raw = staged([P, PACK, T], "x_raw")
+        w1_late = staged([P, PACK, H - W1_EARLY], "w1_late")
         offsets = keep.tile([P, H // 16], U16, name="offsets")
-        w2_raw = kept([P, PACK, N], F32, "w2_raw")
+        w2_raw = staged([P, PACK, N], "w2_raw")
         load(w1_early, w1[:, 0:W1_EARLY])
         load(x_raw, xT)
         load(w1_late, w1[:, W1_EARLY:H])
@@ -160,7 +163,7 @@ def tile_picked_shuffle_mlp_silu_perm_l_kernel(tc, xT, w1, w2, offs, out):
         for b, parts in ((1, w2_grouped[1:2]), (2, w2_grouped[2:3]), (3, last_halves)):
             w2_mx.append(quantize_w2(b, placed([P, P], U8, f"w2_scales{b}", H_GROUPED_AT + (b - 1) * P), parts))
 
-        results = keep.tile([P, N // P, T], F32, name="results")
+        results = staged([P, N // P, T], "results")
         for b, weights in enumerate(w2_mx):
             acc = psum.tile([P, T], F32, name=f"out_acc{b}", tag=f"bank{b}")
             product(acc[:], weights, (h_codes[:], h_scales[:]))

@@ -24,6 +24,7 @@ W1_EARLY = 320
 W1_PIECES = (("vector", 128), ("scalar", 128), ("vector", 64), ("vector", 64), ("scalar", 64), ("vector", 64))
 X_ON_VECTOR = 64
 V_GATHER = 288
+THIRD_ON_VECTOR = 32
 
 
 def tile_picked_shuffle_mlp_silu_perm_l_kernel(tc, xT, w1, w2, offs, out):
@@ -142,8 +143,8 @@ def tile_picked_shuffle_mlp_silu_perm_l_kernel(tc, xT, w1, w2, offs, out):
         last_halves = [kept([P, HALF, PACK], BF16, "w2_grouped3a"), placed([P, HALF, PACK], BF16, "w2_grouped3b", PICKED_AT)]
         round_columns("vector", w2_grouped[0][:], w2_raw[:, :, 0:P])
         round_columns("vector", w2_grouped[1][:], w2_raw[:, :, P : 2 * P])
-        round_columns("vector", w2_grouped[2][:, 0:HALF, :], w2_raw[:, :, 2 * P : 2 * P + HALF])
-        round_columns("scalar", w2_grouped[2][:, HALF:P, :], w2_raw[:, :, 2 * P + HALF : 3 * P])
+        round_columns("vector", w2_grouped[2][:, 0:THIRD_ON_VECTOR, :], w2_raw[:, :, 2 * P : 2 * P + THIRD_ON_VECTOR])
+        round_columns("scalar", w2_grouped[2][:, THIRD_ON_VECTOR:P, :], w2_raw[:, :, 2 * P + THIRD_ON_VECTOR : 3 * P])
         round_columns("scalar", last_halves[0][:], w2_raw[:, :, 3 * P : 3 * P + HALF])
         round_columns("scalar", last_halves[1][:], w2_raw[:, :, 3 * P + HALF : N])
 
@@ -155,19 +156,19 @@ def tile_picked_shuffle_mlp_silu_perm_l_kernel(tc, xT, w1, w2, offs, out):
                 quantize(codes[:, columns], scales[:, columns], grouped[:])
             return codes[:], scales[:]
 
-        w2_mx = [quantize_w2(0, kept([P, P], U8, "w2_scales0"), w2_grouped[0:1])]
+        w2_mx = [quantize_w2(b, kept([P, P], U8, f"w2_scales{b}"), w2_grouped[b : b + 1]) for b in range(2)]
         h_codes = kept([P, T], U32, "h_codes")
         h_scales = kept([P, T], U8, "h_scales")
         for tokens, grouped in zip(halves, h_grouped):
             quantize(h_codes[:, tokens], h_scales[:, tokens], grouped[:])
-        for b, parts in ((1, w2_grouped[1:2]), (2, w2_grouped[2:3]), (3, last_halves)):
+        for b, parts in ((2, w2_grouped[2:3]), (3, last_halves)):
             w2_mx.append(quantize_w2(b, placed([P, P], U8, f"w2_scales{b}", H_GROUPED_AT + (b - 1) * P), parts))
 
         results = staged([P, N // P, T], "results")
         for b, weights in enumerate(w2_mx):
             acc = psum.tile([P, T], F32, name=f"out_acc{b}", tag=f"bank{b}")
             product(acc[:], weights, (h_codes[:], h_scales[:]))
-            copy_on("vector" if b % 2 == 0 else "scalar", results[:, b, :], acc[:])
+            copy_on("scalar" if b == 2 else "vector", results[:, b, :], acc[:])
         rows = out.rearrange("(b p) t -> p b t", p=P)
         for first, last in ((0, 2), (2, 3), (3, 4)):
             nc.sync.dma_start(rows[:, first:last, :], results[:, first:last, :])

@@ -168,7 +168,7 @@ def tile_picked_shuffle_mlp_silu_perm_l_kernel(tc, xT, w1, w2, offs, out):
         for b, weights in enumerate(w2_mx):
             acc = psum.tile([P, T], F32, name=f"out_acc{b}", tag=f"bank{b}")
             product(acc[:], weights, (h_codes[:], h_scales[:]))
-            copy_on("scalar" if b == 2 else "vector", results[:, b, :], acc[:])
+            copy_on("scalar" if b == 1 else "vector", results[:, b, :], acc[:])
         rows = out.rearrange("(b p) t -> p b t", p=P)
-        for first, last in ((0, 2), (2, 3), (3, 4)):
+        for first, last in ((0, 1), (1, 2), (2, 4)):
             nc.sync.dma_start(rows[:, first:last, :], results[:, first:last, :])

@@ -18,13 +18,12 @@ COPY = mybir.ActivationFunctionType.Copy
 P = 128
 PACK = 4
 LINE = 4
-HALF = P // 2
 
 W1_EARLY = 320
 W1_PIECES = (("vector", 128), ("scalar", 128), ("vector", 64), ("vector", 64), ("scalar", 64), ("vector", 64))
 X_ON_VECTOR = 64
 V_GATHER = 288
-THIRD_ON_VECTOR = 32
+W2_ON_VECTOR = (128, 128, 32, 64)
 
 
 def tile_picked_shuffle_mlp_silu_perm_l_kernel(tc, xT, w1, w2, offs, out):
@@ -139,36 +138,32 @@ def tile_picked_shuffle_mlp_silu_perm_l_kernel(tc, xT, w1, w2, offs, out):
                 in_=turned[:].rearrange("p u t -> p t u")[:, tokens, :],
             )
 
-        w2_grouped = [kept([P, P, PACK], BF16, f"w2_grouped{b}") for b in range(3)]
-        last_halves = [kept([P, HALF, PACK], BF16, "w2_grouped3a"), placed([P, HALF, PACK], BF16, "w2_grouped3b", PICKED_AT)]
-        round_columns("vector", w2_grouped[0][:], w2_raw[:, :, 0:P])
-        round_columns("vector", w2_grouped[1][:], w2_raw[:, :, P : 2 * P])
-        round_columns("vector", w2_grouped[2][:, 0:THIRD_ON_VECTOR, :], w2_raw[:, :, 2 * P : 2 * P + THIRD_ON_VECTOR])
-        round_columns("scalar", w2_grouped[2][:, THIRD_ON_VECTOR:P, :], w2_raw[:, :, 2 * P + THIRD_ON_VECTOR : 3 * P])
-        round_columns("scalar", last_halves[0][:], w2_raw[:, :, 3 * P : 3 * P + HALF])
-        round_columns("scalar", last_halves[1][:], w2_raw[:, :, 3 * P + HALF : N])
+        w2_grouped = [kept([P, P, PACK], BF16, f"w2_grouped{b}") for b in range(N // P)]
+        for grouped, c0, on_vector in zip(w2_grouped, (3 * P, 0, P, 2 * P), W2_ON_VECTOR):
+            round_columns("vector", grouped[:, 0:on_vector, :], w2_raw[:, :, c0 : c0 + on_vector])
+            if on_vector < P:
+                round_columns("scalar", grouped[:, on_vector:P, :], w2_raw[:, :, c0 + on_vector : c0 + P])
 
-        def quantize_w2(b, scales, parts):
+        def quantize_w2(b, scales):
             codes = kept([P, P], U32, f"w2_codes{b}")
-            width = P // len(parts)
-            for i, grouped in enumerate(parts):
-                columns = slice(i * width, (i + 1) * width)
-                quantize(codes[:, columns], scales[:, columns], grouped[:])
+            quantize(codes[:], scales[:], w2_grouped[b][:])
             return codes[:], scales[:]
 
-        w2_mx = [quantize_w2(b, kept([P, P], U8, f"w2_scales{b}"), w2_grouped[b : b + 1]) for b in range(2)]
+        w2_mx = [quantize_w2(b, kept([P, P], U8, f"w2_scales{b}")) for b in range(3)]
         h_codes = kept([P, T], U32, "h_codes")
         h_scales = kept([P, T], U8, "h_scales")
         for tokens, grouped in zip(halves, h_grouped):
             quantize(h_codes[:, tokens], h_scales[:, tokens], grouped[:])
-        for b, parts in ((2, w2_grouped[2:3]), (3, last_halves)):
-            w2_mx.append(quantize_w2(b, placed([P, P], U8, f"w2_scales{b}", H_GROUPED_AT + (b - 1) * P), parts))
+        w2_mx.append(quantize_w2(3, placed([P, P], U8, "w2_scales3", H_GROUPED_AT + P)))
 
         results = staged([P, N // P, T], "results")
-        for b, weights in enumerate(w2_mx):
-            acc = psum.tile([P, T], F32, name=f"out_acc{b}", tag=f"bank{b}")
-            product(acc[:], weights, (h_codes[:], h_scales[:]))
-            copy_on("scalar" if b == 1 else "vector", results[:, b, :], acc[:])
+        passes = [(3, w2_mx[0], halves[0], "scalar")]
+        passes += [(b, w2_mx[b + 1], slice(0, T), engine) for b, engine in enumerate(("vector", "scalar", "vector"))]
+        passes += [(3, w2_mx[0], halves[1], "vector")]
+        for i, (b, weights, tokens, engine) in enumerate(passes):
+            acc = psum.tile([P, tokens.stop - tokens.start], F32, name=f"out_acc{i}", tag=f"bank{i}")
+            product(acc[:], weights, (h_codes[:, tokens], h_scales[:, tokens]))
+            copy_on(engine, results[:, b, tokens], acc[:])
         rows = out.rearrange("(b p) t -> p b t", p=P)
         for first, last in ((0, 1), (1, 2), (2, 4)):
             nc.sync.dma_start(rows[:, first:last, :], results[:, first:last, :])

@@ -23,7 +23,7 @@ W1_EARLY = 320
 W1_PIECES = (("vector", 128), ("scalar", 128), ("vector", 64), ("vector", 64), ("scalar", 64), ("vector", 64))
 X_ON_VECTOR = 64
 V_GATHER = 288
-W2_ON_VECTOR = (128, 128, 32, 64)
+W2_ON_SCALAR = 176
 
 
 def tile_picked_shuffle_mlp_silu_perm_l_kernel(tc, xT, w1, w2, offs, out):
@@ -138,32 +138,35 @@ def tile_picked_shuffle_mlp_silu_perm_l_kernel(tc, xT, w1, w2, offs, out):
                 in_=turned[:].rearrange("p u t -> p t u")[:, tokens, :],
             )
 
-        w2_grouped = [kept([P, P, PACK], BF16, f"w2_grouped{b}") for b in range(N // P)]
-        for grouped, c0, on_vector in zip(w2_grouped, (3 * P, 0, P, 2 * P), W2_ON_VECTOR):
-            round_columns("vector", grouped[:, 0:on_vector, :], w2_raw[:, :, c0 : c0 + on_vector])
-            if on_vector < P:
-                round_columns("scalar", grouped[:, on_vector:P, :], w2_raw[:, :, c0 + on_vector : c0 + P])
+        w2_upper = kept([P, N // 2, PACK], BF16, "w2_upper")
+        w2_lower = kept([P, N // 2, PACK], BF16, "w2_lower")
+        round_columns("vector", w2_upper[:], w2_raw[:, :, N // 2 : N])
+        round_columns("vector", w2_lower[:, W2_ON_SCALAR : N // 2, :], w2_raw[:, :, W2_ON_SCALAR : N // 2])
+        round_columns("scalar", w2_lower[:, 0:W2_ON_SCALAR, :], w2_raw[:, :, 0:W2_ON_SCALAR])
 
-        def quantize_w2(b, scales):
-            codes = kept([P, P], U32, f"w2_codes{b}")
-            quantize(codes[:], scales[:], w2_grouped[b][:])
-            return codes[:], scales[:]
-
-        w2_mx = [quantize_w2(b, kept([P, P], U8, f"w2_scales{b}")) for b in range(3)]
+        w2_codes = kept([P, N], U32, "w2_codes")
+        w2_scales = kept([P, N], U8, "w2_scales")
+        quantize(w2_codes[:, N // 2 : N], w2_scales[:, N // 2 : N], w2_upper[:])
+        quantize(w2_codes[:, 0 : N // 2], w2_scales[:, 0 : N // 2], w2_lower[:])
+        w2_mx = [(w2_codes[:, b * P : (b + 1) * P], w2_scales[:, b * P : (b + 1) * P]) for b in range(N // P)]
         h_codes = kept([P, T], U32, "h_codes")
         h_scales = kept([P, T], U8, "h_scales")
         for tokens, grouped in zip(halves, h_grouped):
             quantize(h_codes[:, tokens], h_scales[:, tokens], grouped[:])
-        w2_mx.append(quantize_w2(3, placed([P, P], U8, "w2_scales3", H_GROUPED_AT + P)))
 
         results = staged([P, N // P, T], "results")
-        passes = [(3, w2_mx[0], halves[0], "scalar")]
-        passes += [(b, w2_mx[b + 1], slice(0, T), engine) for b, engine in enumerate(("vector", "scalar", "vector"))]
-        passes += [(3, w2_mx[0], halves[1], "vector")]
-        for i, (b, weights, tokens, engine) in enumerate(passes):
+        whole = slice(0, T)
+        passes = (
+            (2, halves[0], "scalar"),
+            (3, whole, "vector"),
+            (0, whole, "scalar"),
+            (1, whole, "vector"),
+            (2, halves[1], "vector"),
+        )
+        for i, (b, tokens, engine) in enumerate(passes):
             acc = psum.tile([P, tokens.stop - tokens.start], F32, name=f"out_acc{i}", tag=f"bank{i}")
-            product(acc[:], weights, (h_codes[:, tokens], h_scales[:, tokens]))
+            product(acc[:], w2_mx[b], (h_codes[:, tokens], h_scales[:, tokens]))
             copy_on(engine, results[:, b, tokens], acc[:])
         rows = out.rearrange("(b p) t -> p b t", p=P)
-        for first, last in ((0, 1), (1, 2), (2, 4)):
+        for first, last in ((3, 4), (0, 1), (1, 3)):
             nc.sync.dma_start(rows[:, first:last, :], results[:, first:last, :])

@@ -22,8 +22,8 @@ LINE = 4
 W1_EARLY = 320
 W1_PIECES = (("vector", 128), ("scalar", 128), ("vector", 64), ("vector", 64), ("scalar", 64), ("vector", 64))
 X_ON_VECTOR = 64
-V_GATHER = 288
-W2_ON_SCALAR = 176
+V_GATHER = 256
+W2_ON_SCALAR = 160
 
 
 def tile_picked_shuffle_mlp_silu_perm_l_kernel(tc, xT, w1, w2, offs, out):

@@ -34,10 +34,10 @@ def tile_picked_shuffle_mlp_silu_perm_l_kernel(tc, xT, w1, w2, offs, out):
         psum = ctx.enter_context(tc.psum_pool(name="psum", bufs=1))
 
         def kept(shape, dtype, name):
-            return keep.tile(shape, dtype, name=name, align_bytes=64)
+            return keep.tile(shape, dtype, name=name, align_bytes=256)
 
         def placed(shape, dtype, name, offset):
-            return reuse.tile(shape, dtype, name=name, offset=offset, align_bytes=64)
+            return reuse.tile(shape, dtype, name=name, offset=offset, align_bytes=256)
 
         def staged(shape, name):
             return keep.tile(shape, F32, name=name, align_bytes=256)
@@ -77,7 +77,7 @@ def tile_picked_shuffle_mlp_silu_perm_l_kernel(tc, xT, w1, w2, offs, out):
         w1_early = staged([P, PACK, W1_EARLY], "w1_early")
         x_raw = staged([P, PACK, T], "x_raw")
         w1_late = staged([P, PACK, H - W1_EARLY], "w1_late")
-        offsets = keep.tile([P, H // 16], U16, name="offsets")
+        offsets = kept([P, H // 16], U16, "offsets")
         w2_raw = staged([P, PACK, N], "w2_raw")
         load(w1_early, w1[:, 0:W1_EARLY])
         load(x_raw, xT)
@@ -88,7 +88,7 @@ def tile_picked_shuffle_mlp_silu_perm_l_kernel(tc, xT, w1, w2, offs, out):
         warm = keep.tile([P, 1], F32, name="warm")
         nc.vector.memset(warm[:], 0.0)
         nc.scalar.activation(warm[:], warm[:], SILU)
-        ident = keep.tile([P, P], F32, name="ident")
+        ident = kept([P, P], F32, "ident")
         make_identity(nc, ident[:])
 
         x_grouped = kept([P, T, PACK], BF16, "x_grouped")

@@ -23,7 +23,7 @@ W1_EARLY = 320
 W1_PIECES = (("vector", 128), ("scalar", 128), ("vector", 64), ("vector", 64), ("scalar", 64), ("vector", 64))
 X_ON_VECTOR = 64
 V_GATHER = 256
-W2_ON_SCALAR = 160
+W2_ON_SCALAR = 192
 
 
 def tile_picked_shuffle_mlp_silu_perm_l_kernel(tc, xT, w1, w2, offs, out):

from contextlib import ExitStack

import concourse.mybir as mybir
from concourse.masks import make_identity

K, T, H, N = 512, 128, 512, 512
FLOPS = 2 * T * H * (K + N)

F32 = mybir.dt.float32
BF16 = mybir.dt.bfloat16
U32 = mybir.dt.uint32
U16 = mybir.dt.uint16
U8 = mybir.dt.uint8
FP8X4 = mybir.dt.float8_e4m3fn_x4
SILU = mybir.ActivationFunctionType.Silu
COPY = mybir.ActivationFunctionType.Copy

P = 128
PACK = 4
LINE = 4

W1_EARLY = 320
W1_PIECES = (("vector", 128), ("scalar", 128), ("vector", 64), ("vector", 64), ("scalar", 64), ("vector", 64))
X_ON_VECTOR = 64
V_GATHER = 256
W2_ON_SCALAR = 192


def tile_picked_shuffle_mlp_silu_perm_l_kernel(tc, xT, w1, w2, offs, out):
    nc = tc.nc
    with ExitStack() as ctx:
        keep = ctx.enter_context(tc.tile_pool(name="keep", bufs=1))
        reuse = ctx.enter_context(tc.tile_pool(name="reuse", bufs=1))
        psum = ctx.enter_context(tc.psum_pool(name="psum", bufs=1))

        def kept(shape, dtype, name):
            return keep.tile(shape, dtype, name=name, align_bytes=256)

        def placed(shape, dtype, name, offset):
            return reuse.tile(shape, dtype, name=name, offset=offset, align_bytes=256)

        def staged(shape, name):
            return keep.tile(shape, F32, name=name, align_bytes=256)

        def load(raw, dram):
            nc.sync.dma_start(raw[:], dram.rearrange("(p j) w -> p j w", j=PACK))

        def copy_on(engine, dst, src):
            if engine == "vector":
                nc.vector.tensor_copy(out=dst, in_=src)
            else:
                nc.scalar.copy(out=dst, in_=src)

        def round_columns(engine, grouped, raw):
            copy_on(
                engine,
                grouped.rearrange("p (c i) j -> p c j i", i=LINE),
                raw.rearrange("p j (c i) -> p c j i", i=LINE),
            )

        def quantize(codes, scales, grouped):
            nc.vector.quantize_mx(out=codes.bitcast(FP8X4), scales=scales, in_=grouped.rearrange("p w j -> p (w j)"))

        def product(acc, stationary, moving):
            nc.tensor.matmul_mx(
                out=acc,
                lhsT=stationary[0].bitcast(FP8X4),
                lhsT_scale=stationary[1],
                rhs=moving[0].bitcast(FP8X4),
                rhs_scale=moving[1],
                start=True,
                stop=True,
            )

        H_GROUPED_AT, PICKED_AT = 0, 1024

        w1_early = staged([P, PACK, W1_EARLY], "w1_early")
        x_raw = staged([P, PACK, T], "x_raw")
        w1_late = staged([P, PACK, H - W1_EARLY], "w1_late")
        offsets = kept([P, H // 16], U16, "offsets")
        w2_raw = staged([P, PACK, N], "w2_raw")
        load(w1_early, w1[:, 0:W1_EARLY])
        load(x_raw, xT)
        load(w1_late, w1[:, W1_EARLY:H])
        nc.sync.dma_start(offsets[:], offs)
        load(w2_raw, w2)

        warm = keep.tile([P, 1], F32, name="warm")
        nc.vector.memset(warm[:], 0.0)
        nc.scalar.activation(warm[:], warm[:], SILU)
        ident = kept([P, P], F32, "ident")
        make_identity(nc, ident[:])

        x_grouped = kept([P, T, PACK], BF16, "x_grouped")
        round_columns("vector", x_grouped[:, 0:X_ON_VECTOR, :], x_raw[:, :, 0:X_ON_VECTOR])
        round_columns("scalar", x_grouped[:, X_ON_VECTOR:T, :], x_raw[:, :, X_ON_VECTOR:T])
        w1_grouped = []
        c0 = 0
        for engine, width in W1_PIECES:
            grouped = kept([P, width, PACK], BF16, f"w1_grouped{c0}")
            if c0 < W1_EARLY:
                raw = w1_early[:, :, c0 : c0 + width]
            else:
                raw = w1_late[:, :, c0 - W1_EARLY : c0 - W1_EARLY + width]
            round_columns(engine, grouped[:], raw)
            w1_grouped.append((c0, width, grouped))
            c0 += width

        x_codes = kept([P, T], U32, "x_codes")
        x_scales = kept([P, T], U8, "x_scales")
        quantize(x_codes[:], x_scales[:], x_grouped[:])
        w1_mx = []
        for c0, width, grouped in w1_grouped:
            codes = kept([P, width], U32, f"w1_codes{c0}")
            scales = kept([P, width], U8, f"w1_scales{c0}")
            quantize(codes[:], scales[:], grouped[:])
            w1_mx.append((c0, width, codes, scales))

        h = kept([P, H], BF16, "h")
        for i, (c0, width, codes, scales) in enumerate(w1_mx):
            acc = psum.tile([P, width], F32, name=f"acc{i}", tag=f"bank{i}")
            product(acc[:], (x_codes[:], x_scales[:]), (codes[:], scales[:]))
            nc.scalar.activation(h[:, c0 : c0 + width], acc[:], SILU)

        picked = placed([P, H], BF16, "picked", PICKED_AT)
        nc.vector.tensor_copy(picked[:, 0:V_GATHER], h[:].indirect(offsets[:, 0 : V_GATHER // 16]))
        nc.scalar.activation(picked[:, V_GATHER:H], h[:].indirect(offsets[:, V_GATHER // 16 : H // 16]), COPY)

        turned = psum.tile([P, 2, T], F32, name="turned")
        words = picked[:].bitcast(F32)
        for u in range(2):
            nc.tensor.transpose(turned[:, u, :], words[:, u : H // 2 : 2], ident[:])
        halves = (slice(0, T // 2), slice(T // 2, T))
        h_grouped = [placed([P, T // 2, PACK], BF16, "h_grouped0", H_GROUPED_AT), kept([P, T // 2, PACK], BF16, "h_grouped1")]
        for tokens, grouped in zip(halves, h_grouped):
            nc.scalar.copy(
                out=grouped[:].rearrange("p t j -> p (t j)").bitcast(F32).rearrange("p (t u) -> p t u", u=2),
                in_=turned[:].rearrange("p u t -> p t u")[:, tokens, :],
            )

        w2_upper = kept([P, N // 2, PACK], BF16, "w2_upper")
        w2_lower = kept([P, N // 2, PACK], BF16, "w2_lower")
        round_columns("vector", w2_upper[:], w2_raw[:, :, N // 2 : N])
        round_columns("vector", w2_lower[:, W2_ON_SCALAR : N // 2, :], w2_raw[:, :, W2_ON_SCALAR : N // 2])
        round_columns("scalar", w2_lower[:, 0:W2_ON_SCALAR, :], w2_raw[:, :, 0:W2_ON_SCALAR])

        w2_codes = kept([P, N], U32, "w2_codes")
        w2_scales = kept([P, N], U8, "w2_scales")
        quantize(w2_codes[:, N // 2 : N], w2_scales[:, N // 2 : N], w2_upper[:])
        quantize(w2_codes[:, 0 : N // 2], w2_scales[:, 0 : N // 2], w2_lower[:])
        w2_mx = [(w2_codes[:, b * P : (b + 1) * P], w2_scales[:, b * P : (b + 1) * P]) for b in range(N // P)]
        h_codes = kept([P, T], U32, "h_codes")
        h_scales = kept([P, T], U8, "h_scales")
        for tokens, grouped in zip(halves, h_grouped):
            quantize(h_codes[:, tokens], h_scales[:, tokens], grouped[:])

        results = staged([P, N // P, T], "results")
        whole = slice(0, T)
        passes = (
            (2, halves[0], "scalar"),
            (3, whole, "vector"),
            (0, whole, "scalar"),
            (1, whole, "vector"),
            (2, halves[1], "vector"),
        )
        for i, (b, tokens, engine) in enumerate(passes):
            acc = psum.tile([P, tokens.stop - tokens.start], F32, name=f"out_acc{i}", tag=f"bank{i}")
            product(acc[:], w2_mx[b], (h_codes[:, tokens], h_scales[:, tokens]))
            copy_on(engine, results[:, b, tokens], acc[:])
        rows = out.rearrange("(b p) t -> p b t", p=P)
        for first, last in ((3, 4), (0, 1), (1, 3)):
            nc.sync.dma_start(rows[:, first:last, :], results[:, first:last, :])
